import numpy as np
import ml_dtypes


def mxq(x, axis, fmt="e4m3"):
    dtype, down = {"e4m3": (ml_dtypes.float8_e4m3fn, 7), "e5m2": (ml_dtypes.float8_e5m2, 14)}[fmt]
    v = np.moveaxis(np.asarray(x, np.float32).astype(ml_dtypes.bfloat16).astype(np.float64), axis, -1)
    blocks = v.reshape(v.shape[:-1] + (-1, 32))
    amax = np.abs(blocks).max(-1, keepdims=True)
    byte = np.maximum(np.where(amax > 0, np.frexp(amax)[1] - 1 + 127, 0) - down, 1)
    scale = np.exp2(byte - 127.0)
    codes = (blocks / scale).astype(np.float32).astype(dtype).astype(np.float64)
    return np.moveaxis((codes * scale).reshape(v.shape), -1, axis)


WIDE = False


def mx_kscale(k):
    if not WIDE:
        return np.ones(k)
    levels = np.array([10, -10, 5, -5, 0])
    if k % 512:
        return np.exp2(np.random.permutation(np.resize(levels, k // 32))).repeat(32)
    a = np.empty((k // 512, 16))
    for p in range(k // 512):
        a[p, :8] = np.random.permutation(np.resize(levels, 8))
        for g in range(8):
            far = levels[np.abs(levels - a[p, g]) >= 10]
            a[p, g + 8] = far[np.random.randint(len(far))]
    return np.exp2(a.ravel()).repeat(32)


def f64(x):
    return np.asarray(x).astype(np.float64)


def striped(idx):
    return np.tile(idx.reshape(-1, 16).T, (8, 1)).astype(np.uint16)


def unstriped(offs):
    return offs[:16].T.reshape(-1).astype(np.int64)


def relu(v):
    return np.maximum(v, 0.0)

def planes(y):
    n, m = y.shape
    v = y.astype(np.float32).astype(ml_dtypes.bfloat16).astype(np.float64).reshape(n // 32, 32, m)
    top = np.abs(v).max(1)
    byte = np.clip(np.where(top > 0, np.frexp(top)[1] - 1 + 127 - 7, 1), 1, 254)
    codes = (v * np.exp2(127.0 - byte)[:, None, :]).reshape(n, m).astype(np.float32).astype(ml_dtypes.float8_e4m3fn).view(np.uint8)
    words = codes.reshape(n // 512, 128, 4, m).transpose(0, 1, 3, 2)
    return np.ascontiguousarray(words), np.ascontiguousarray(byte.astype(np.uint8).reshape(n // 512, 16, m))


K, T, S, D, V, H, U = 512, 2048, 512, 4, 512, 512, 1024
P = 2 ** 7


def setup_inputs():
    n = np.random.standard_normal
    s = mx_kscale(K)[:, None]
    u = mx_kscale(H)
    return {
        "xT": (n((K, T)) * s).astype(np.float32),
        "w1": (n((K, H)) / np.sqrt(K) / s * u).astype(np.float32),
        "w2": (n((H, H)) / np.sqrt(H) / u[:, None]).astype(np.float32),
        "gate": np.tile(np.random.uniform(0.2, 0.6, (D, 1, V)), (1, P, 1)).astype(np.float32),
        "emb": (0.5 * n((H, U)) * u[:, None]).astype(np.float32),
        "offs": striped(np.random.permutation(T)[:S]),
        "cell": striped(np.random.permutation(U)[:S]),
        "pos1": striped(np.random.permutation(U)[:V]),
        "pos2": striped(np.random.permutation(U)[:V]),
        "pos3": striped(np.random.permutation(U)[:V]),
        "pos4": striped(np.random.permutation(U)[:V]),
    }


def reference(xT, w1, w2, gate, emb, offs, cell, pos1, pos2, pos3, pos4):
    xq = mxq(f64(xT)[:, unstriped(offs)], 0, "e4m3")
    up = np.zeros((H, U))
    up[:, unstriped(cell)] = relu(mxq(f64(w1), 0, "e4m3").T @ xq)
    z = up + f64(emb)
    y = mxq(f64(w2), 0, "e4m3").T @ mxq(z, 0, "e4m3")
    out_0 = y[:, unstriped(pos1)] * f64(gate)[0, :1] + y[:, unstriped(pos2)] * f64(gate)[1, :1] + y[:, unstriped(pos3)] * f64(gate)[2, :1] + y[:, unstriped(pos4)] * f64(gate)[3, :1]
    return (out_0,) + planes(out_0)

@@ -1,0 +1,223 @@
+from contextlib import ExitStack
+
+import concourse.mybir as mybir
+
+K, T, S, D, V, H, U = 512, 2048, 512, 4, 512, 512, 1024
+FLOPS = 2 * K * H * S + 2 * H * H * U
+
+F32 = mybir.dt.float32
+BF16 = mybir.dt.bfloat16
+I32 = mybir.dt.int32
+U32 = mybir.dt.uint32
+U16 = mybir.dt.uint16
+U8 = mybir.dt.uint8
+FP8X4 = mybir.dt.float8_e4m3fn_x4
+ACT = mybir.ActivationFunctionType
+ALU = mybir.AluOpType
+
+P = 128
+PACK = 4
+HALF = 256
+BANK = 512
+W1_VECTOR_ROWS = 84
+
+
+def tile_picked_devox_none_lo_kernel(
+    tc, xT, w1, w2, gate, emb, offs, cell, pos1, pos2, pos3, pos4, out_0, out_1, out_2
+):
+    nc = tc.nc
+    with ExitStack() as ctx:
+        lists = ctx.enter_context(tc.tile_pool(name="lists", bufs=1))
+        sb = ctx.enter_context(tc.tile_pool(name="sb", bufs=1))
+        ps = ctx.enter_context(tc.psum_pool(name="ps", bufs=1))
+
+        def load_list(src, name):
+            held = lists.tile([P, S // 16], U16, name=name)
+            nc.sync.dma_start(held[:], src)
+            return held
+
+        def tiles(shape, dtype, name, count):
+            return [sb.tile(shape, dtype, name=name + str(i), align_bytes=64) for i in range(count)]
+
+        def entries(held, first, count):
+            return held[:, first // 16 : (first + count) // 16]
+
+        def quantize(codes, scales, grouped):
+            nc.vector.quantize_mx(out=codes.bitcast(FP8X4), scales=scales, in_=grouped)
+
+        def product(bank, w_codes, w_scales, t, codes, scales):
+            cols = slice(t * P, (t + 1) * P)
+            nc.tensor.matmul_mx(
+                out=bank,
+                lhsT=w_codes[:, cols].bitcast(FP8X4),
+                lhsT_scale=w_scales[:, cols],
+                rhs=codes.bitcast(FP8X4),
+                rhs_scale=scales,
+                start=True,
+                stop=True,
+            )
+
+        def dealt(grouped, raw, m0, m1):
+            return (
+                grouped[:].rearrange("p (t m j) -> p m t j", t=PACK, j=PACK)[:, m0:m1],
+                raw[:].rearrange("p j (m t) -> p m t j", t=PACK)[:, m0:m1],
+            )
+
+        def woven(grouped, planes):
+            return (
+                grouped.rearrange("p (c i t) -> p c t i", i=4, t=PACK),
+                planes.rearrange("p t (c i) -> p c t i", i=4),
+            )
+
+        offs_sb = load_list(offs, "offs")
+        x_rows = xT.rearrange("(p t) c -> t p c", t=PACK)
+        x_sb = tiles([P, T], F32, "x", PACK)
+        for t in range(PACK):
+            nc.sync.dma_start(x_sb[t][:], x_rows[t])
+        w1_raw = sb.tile([P, PACK, H], F32, name="w1_raw")
+        nc.sync.dma_start(w1_raw[:], w1.rearrange("(p j) c -> p j c", j=PACK))
+        cell_sb = load_list(cell, "cell")
+        w2_raw = sb.tile([P, PACK, H], F32, name="w2_raw")
+        nc.sync.dma_start(w2_raw[:], w2.rearrange("(p j) c -> p j c", j=PACK))
+        emb_rows = emb.rearrange("(p t) c -> t p c", t=PACK)
+        emb_sb = tiles([P, U], F32, "emb", PACK)
+        for t in range(PACK):
+            nc.sync.dma_start(emb_sb[t][:], emb_rows[t])
+        pos_sb = [load_list(src, "pos" + str(d)) for d, src in enumerate((pos1, pos2, pos3, pos4))]
+        gate_sb = sb.tile([P, D, V], F32, name="gate_sb")
+        nc.sync.dma_start(gate_sb[:], gate.rearrange("d p v -> p d v"))
+
+        up = tiles([P, U], F32, "up", PACK)
+        for t in range(PACK):
+            nc.gpsimd.memset(up[t][:], 0.0)
+
+        x_grouped = sb.tile([P, S, PACK], BF16, name="x_grouped", align_bytes=64)
+        for t in range(PACK):
+            nc.vector.tensor_copy(x_grouped[:, :, t], x_sb[t][:].indirect(offs_sb[:]))
+        x_codes = sb.tile([P, S], U32, name="x_codes", align_bytes=64)
+        x_scales = sb.tile([P, S], U8, name="x_scales", align_bytes=64)
+        quantize(x_codes[:], x_scales[:], x_grouped[:].rearrange("p c t -> p (c t)"))
+
+        w1_grouped = sb.tile([P, PACK * H], BF16, name="w1_grouped", align_bytes=64)
+        nc.vector.tensor_copy(*dealt(w1_grouped, w1_raw, 0, W1_VECTOR_ROWS))
+        nc.scalar.copy(*dealt(w1_grouped, w1_raw, W1_VECTOR_ROWS, P))
+        w1_codes = sb.tile([P, H], U32, name="w1_codes", align_bytes=64)
+        w1_scales = sb.tile([P, H], U8, name="w1_scales", align_bytes=64)
+        banks = [ps.tile([P, BANK], F32, name="bank" + str(b)) for b in range(8)]
+        for t in (1, 0, 2, 3):
+            cols = slice(t * P, (t + 1) * P)
+            quantize(w1_codes[:, cols], w1_scales[:, cols], w1_grouped[:, t * H : (t + 1) * H])
+            product(banks[t][:], w1_codes, w1_scales, t, x_codes[:], x_scales[:])
+
+        h = tiles([P, S], F32, "h", PACK)
+
+        def scatter_scalar(t, first):
+            nc.scalar.activation(
+                up[t][:].indirect(entries(cell_sb, first, HALF)), h[t][:, first : first + HALF], ACT.Copy
+            )
+
+        nc.scalar.activation(h[1][:], banks[1][:], ACT.Relu)
+        scatter_scalar(1, 0)
+        scatter_scalar(1, HALF)
+        nc.vector.tensor_scalar_max(h[0][:], banks[0][:], 0.0)
+        nc.vector.tensor_scalar_max(h[3][:], banks[3][:], 0.0)
+        nc.vector.tensor_copy(up[0][:].indirect(cell_sb[:]), h[0][:])
+        nc.scalar.activation(h[2][:], banks[2][:], ACT.Relu)
+        scatter_scalar(2, 0)
+        scatter_scalar(2, HALF)
+        nc.vector.tensor_copy(up[3][:].indirect(entries(cell_sb, 0, HALF)), h[3][:, 0:HALF])
+        scatter_scalar(3, HALF)
+
+        w2_grouped = sb.tile([P, PACK * H], BF16, name="w2_grouped", align_bytes=64)
+        w2_out, w2_in = dealt(w2_grouped, w2_raw, 0, P)
+        nc.gpsimd.tensor_scalar(w2_out, w2_in, 1.0, 0.0, ALU.mult, ALU.add)
+        w2_codes = sb.tile([P, H], U32, name="w2_codes", align_bytes=64)
+        w2_scales = sb.tile([P, H], U8, name="w2_scales", align_bytes=64)
+
+        z_planes = tiles([P, PACK, BANK], BF16, "z_planes", 2)
+        z_grouped = tiles([P, PACK * BANK], BF16, "z_grouped", 2)
+        z_codes = tiles([P, BANK], U32, "z_codes", 2)
+        z_scales = tiles([P, BANK], U8, "z_scales", 2)
+
+        def add_emb(t, half):
+            cols = slice(half * BANK, (half + 1) * BANK)
+            nc.vector.tensor_tensor(z_planes[half][:, t, :], up[t][:, cols], emb_sb[t][:, cols], ALU.add)
+
+        for t in (0, 1):
+            add_emb(t, 0)
+            add_emb(t, 1)
+        quantize(w2_codes[:], w2_scales[:], w2_grouped[:])
+        for t in (2, 3):
+            add_emb(t, 0)
+        for t in (2, 3):
+            add_emb(t, 1)
+        nc.vector.tensor_copy(*woven(z_grouped[0][:], z_planes[0][:]))
+        nc.scalar.copy(*woven(z_grouped[1][:, 0:1024], z_planes[1][:, :, 0:256]))
+        nc.vector.tensor_copy(*woven(z_grouped[1][:, 1024:2048], z_planes[1][:, :, 256:512]))
+        y = tiles([P, U], F32, "y", PACK)
+        for half in (0, 1):
+            quantize(z_codes[half][:], z_scales[half][:], z_grouped[half][:])
+            for t in range(PACK):
+                bank = banks[4 * (1 - half) + t]
+                product(bank[:], w2_codes, w2_scales, t, z_codes[half][:], z_scales[half][:])
+        for t in range(PACK):
+            nc.scalar.copy(y[t][:, 0:BANK], banks[4 + t][:])
+
+        terms = tiles([P, D, V], F32, "terms", PACK)
+        pairs = tiles([P, 2, V], F32, "pairs", 2)
+        result = tiles([P, PACK, HALF], F32, "result", 2)
+        out_rows = out_0.rearrange("(p t) v -> p t v", t=PACK)
+        o_grouped = tiles([P, PACK * HALF], BF16, "o_grouped", 2)
+        o_codes = sb.tile([P, V], U32, name="o_codes", align_bytes=64)
+        o_scales = sb.tile([P, V], U8, name="o_scales", align_bytes=64)
+        words_out = out_1.rearrange("z p c r -> p (z c r)").bitcast(I32)
+        scales_out = out_2.rearrange("z q c -> (z q) c").bitcast(I32)
+
+        def fetch_weighted(t):
+            for d in range(D):
+                nc.vector.tensor_tensor(terms[t][:, d, :], y[t][:].indirect(pos_sb[d][:]), gate_sb[:, d, :], ALU.mult)
+
+        def fetch(t, first, count):
+            cols = slice(first, first + count)
+            for d in range(D):
+                nc.scalar.activation(terms[t][:, d, cols], y[t][:].indirect(entries(pos_sb[d], first, count)), ACT.Copy)
+
+        def weigh(t, first, count):
+            cols = slice(first, first + count)
+            nc.vector.tensor_tensor(terms[t][:, :, cols], terms[t][:, :, cols], gate_sb[:, :, cols], ALU.mult)
+
+        def add_up(t, first, count):
+            cols = slice(first, first + count)
+            nc.vector.tensor_tensor(pairs[t % 2][:, :, cols], terms[t][:, 0:2, cols], terms[t][:, 2:D, cols], ALU.add)
+            for half in range(first // HALF, (first + count) // HALF):
+                part = slice(half * HALF, (half + 1) * HALF)
+                nc.vector.tensor_tensor(result[half][:, t, :], pairs[t % 2][:, 0, part], pairs[t % 2][:, 1, part], ALU.add)
+                nc.sync.dma_start(out_rows[:, t, part], result[half][:, t, :])
+
+        def hand_on(half):
+            part = slice(half * HALF, (half + 1) * HALF)
+            quantize(o_codes[:, part], o_scales[:, part], o_grouped[half][:])
+            nc.sync.dma_start(words_out[:, part], o_codes[:, part].bitcast(I32))
+
+        nc.vector.tensor_copy(y[0][:, BANK:U], banks[0][:])
+        fetch_weighted(0)
+        add_up(0, 0, V)
+        for t in (1, 2):
+            nc.scalar.copy(y[t][:, BANK:U], banks[t][:])
+            fetch(t, 0, V)
+            weigh(t, 0, V)
+            add_up(t, 0, V)
+        nc.scalar.copy(y[3][:, BANK:U], banks[3][:])
+        fetch(3, 0, HALF)
+        fetch(3, HALF, HALF)
+        weigh(3, 0, HALF)
+        add_up(3, 0, HALF)
+        nc.scalar.copy(*woven(o_grouped[0][:], result[0][:]))
+        weigh(3, HALF, HALF)
+        add_up(3, HALF, HALF)
+        nc.vector.tensor_copy(*woven(o_grouped[1][:], result[1][:]))
+        hand_on(0)
+        hand_on(1)
+        for q in range(4):
+            queue = nc.scalar if q % 2 else nc.sync
+            queue.dma_start(scales_out[4 * q : 4 * q + 4, :], o_scales[32 * q : 32 * q + 4, :].bitcast(I32))

@@ -1,6 +1,7 @@
 from contextlib import ExitStack
 
 import concourse.mybir as mybir
+from concourse.masks import make_identity
 
 K, T, S, D, V, H, U = 512, 2048, 512, 4, 512, 512, 1024
 FLOPS = 2 * K * H * S + 2 * H * H * U
@@ -20,6 +21,7 @@ PACK = 4
 HALF = 256
 BANK = 512
 W1_VECTOR_ROWS = 84
+ROUND_VECTOR_COLUMNS = 320
 
 
 def tile_picked_devox_none_lo_kernel(
@@ -37,7 +39,7 @@ def tile_picked_devox_none_lo_kernel(
             return held
 
         def tiles(shape, dtype, name, count):
-            return [sb.tile(shape, dtype, name=name + str(i), align_bytes=64) for i in range(count)]
+            return [sb.tile(shape, dtype, name=name + str(i), tag=name + str(i), align_bytes=64) for i in range(count)]
 
         def entries(held, first, count):
             return held[:, first // 16 : (first + count) // 16]
@@ -91,6 +93,9 @@ def tile_picked_devox_none_lo_kernel(
         for t in range(PACK):
             nc.gpsimd.memset(up[t][:], 0.0)
 
+        identity = sb.tile([P, P], F32, name="identity")
+        make_identity(nc, identity[:])
+
         x_grouped = sb.tile([P, S, PACK], BF16, name="x_grouped", align_bytes=64)
         for t in range(PACK):
             nc.vector.tensor_copy(x_grouped[:, :, t], x_sb[t][:].indirect(offs_sb[:]))
@@ -104,7 +109,7 @@ def tile_picked_devox_none_lo_kernel(
         w1_codes = sb.tile([P, H], U32, name="w1_codes", align_bytes=64)
         w1_scales = sb.tile([P, H], U8, name="w1_scales", align_bytes=64)
         banks = [ps.tile([P, BANK], F32, name="bank" + str(b)) for b in range(8)]
-        for t in (1, 0, 2, 3):
+        for t in range(PACK):
             cols = slice(t * P, (t + 1) * P)
             quantize(w1_codes[:, cols], w1_scales[:, cols], w1_grouped[:, t * H : (t + 1) * H])
             product(banks[t][:], w1_codes, w1_scales, t, x_codes[:], x_scales[:])
@@ -120,22 +125,23 @@ def tile_picked_devox_none_lo_kernel(
         scatter_scalar(1, 0)
         scatter_scalar(1, HALF)
         nc.vector.tensor_scalar_max(h[0][:], banks[0][:], 0.0)
-        nc.vector.tensor_scalar_max(h[3][:], banks[3][:], 0.0)
         nc.vector.tensor_copy(up[0][:].indirect(cell_sb[:]), h[0][:])
+        nc.vector.tensor_scalar_max(h[3][:], banks[3][:], 0.0)
         nc.scalar.activation(h[2][:], banks[2][:], ACT.Relu)
         scatter_scalar(2, 0)
         scatter_scalar(2, HALF)
         nc.vector.tensor_copy(up[3][:].indirect(entries(cell_sb, 0, HALF)), h[3][:, 0:HALF])
         scatter_scalar(3, HALF)
 
-        w2_grouped = sb.tile([P, PACK * H], BF16, name="w2_grouped", align_bytes=64)
-        w2_out, w2_in = dealt(w2_grouped, w2_raw, 0, P)
-        nc.gpsimd.tensor_scalar(w2_out, w2_in, 1.0, 0.0, ALU.mult, ALU.add)
+        w2_dealt = w2_raw[:].rearrange("p j (m t) -> p m t j", t=PACK)
+        w2_first = sb.tile([P, H], BF16, name="w2_first", tag="h3", align_bytes=64)
+        nc.scalar.copy(w2_first[:].rearrange("p (m j) -> p m j", j=PACK), w2_dealt[:, :, 0, :])
         w2_codes = sb.tile([P, H], U32, name="w2_codes", align_bytes=64)
         w2_scales = sb.tile([P, H], U8, name="w2_scales", align_bytes=64)
 
         z_planes = tiles([P, PACK, BANK], BF16, "z_planes", 2)
-        z_grouped = tiles([P, PACK * BANK], BF16, "z_grouped", 2)
+        z_quarter = tiles([P, PACK * HALF], BF16, "z_quarter", 2)
+        z_half = sb.tile([P, PACK * BANK], BF16, name="z_half", align_bytes=64)
         z_codes = tiles([P, BANK], U32, "z_codes", 2)
         z_scales = tiles([P, BANK], U8, "z_scales", 2)
 
@@ -143,81 +149,101 @@ def tile_picked_devox_none_lo_kernel(
             cols = slice(half * BANK, (half + 1) * BANK)
             nc.vector.tensor_tensor(z_planes[half][:, t, :], up[t][:, cols], emb_sb[t][:, cols], ALU.add)
 
-        for t in (0, 1):
-            add_emb(t, 0)
-            add_emb(t, 1)
-        quantize(w2_codes[:], w2_scales[:], w2_grouped[:])
-        for t in (2, 3):
-            add_emb(t, 0)
-        for t in (2, 3):
-            add_emb(t, 1)
-        nc.vector.tensor_copy(*woven(z_grouped[0][:], z_planes[0][:]))
-        nc.scalar.copy(*woven(z_grouped[1][:, 0:1024], z_planes[1][:, :, 0:256]))
-        nc.vector.tensor_copy(*woven(z_grouped[1][:, 1024:2048], z_planes[1][:, :, 256:512]))
-        y = tiles([P, U], F32, "y", PACK)
-        for half in (0, 1):
-            quantize(z_codes[half][:], z_scales[half][:], z_grouped[half][:])
-            for t in range(PACK):
-                bank = banks[4 * (1 - half) + t]
-                product(bank[:], w2_codes, w2_scales, t, z_codes[half][:], z_scales[half][:])
         for t in range(PACK):
-            nc.scalar.copy(y[t][:, 0:BANK], banks[4 + t][:])
+            add_emb(t, 0)
+            add_emb(t, 1)
+        quantize(w2_codes[:, 0:P], w2_scales[:, 0:P], w2_first[:])
+        quarters = [slice(0, HALF), slice(HALF, BANK)]
+        for i in (0, 1):
+            nc.scalar.copy(*woven(z_quarter[i][:], z_planes[0][:, :, quarters[i]]))
+        nc.vector.tensor_copy(*woven(z_half[:], z_planes[1][:]))
+        w2_rest = sb.tile([P, (PACK - 1) * H], BF16, name="w2_rest", tag="z_planes0", align_bytes=64)
+        nc.scalar.copy(w2_rest[:].rearrange("p (t m j) -> p m t j", t=PACK - 1, j=PACK), w2_dealt[:, :, 1:PACK, :])
+        y = tiles([P, U], F32, "y", PACK)
+        quantize(z_codes[0][:, quarters[0]], z_scales[0][:, quarters[0]], z_quarter[0][:])
+        product(banks[0][:, 0:HALF], w2_codes, w2_scales, 0, z_codes[0][:, quarters[0]], z_scales[0][:, quarters[0]])
+        quantize(z_codes[1][:], z_scales[1][:], z_half[:])
+        product(banks[4][:], w2_codes, w2_scales, 0, z_codes[1][:], z_scales[1][:])
+        quantize(z_codes[0][:, quarters[1]], z_scales[0][:, quarters[1]], z_quarter[1][:])
+        product(banks[3][:, 0:HALF], w2_codes, w2_scales, 0, z_codes[0][:, quarters[1]], z_scales[0][:, quarters[1]])
+        nc.vector.tensor_copy(y[0][:, quarters[0]], banks[0][:, 0:HALF])
+        nc.vector.tensor_copy(y[0][:, BANK:U], banks[4][:])
+        nc.scalar.copy(y[0][:, quarters[1]], banks[3][:, 0:HALF])
+        quantize(w2_codes[:, P:H], w2_scales[:, P:H], w2_rest[:])
+        for t in range(1, PACK):
+            for half in (1, 0):
+                product(banks[4 * half + t][:], w2_codes, w2_scales, t, z_codes[half][:], z_scales[half][:])
+
+        def y_out(t, half):
+            return y[t][:, half * BANK : (half + 1) * BANK], banks[4 * half + t][:]
 
         terms = tiles([P, D, V], F32, "terms", PACK)
-        pairs = tiles([P, 2, V], F32, "pairs", 2)
-        result = tiles([P, PACK, HALF], F32, "result", 2)
+        pairs = sb.tile([P, 2, V], F32, name="pairs")
+        turned = tiles([P, V], F32, "turned", PACK - 1)
+        result = sb.tile([P, PACK, V], F32, name="result")
         out_rows = out_0.rearrange("(p t) v -> p t v", t=PACK)
-        o_grouped = tiles([P, PACK * HALF], BF16, "o_grouped", 2)
+        o_grouped = sb.tile([P, PACK * V], BF16, name="o_grouped", align_bytes=64)
         o_codes = sb.tile([P, V], U32, name="o_codes", align_bytes=64)
         o_scales = sb.tile([P, V], U8, name="o_scales", align_bytes=64)
         words_out = out_1.rearrange("z p c r -> p (z c r)").bitcast(I32)
         scales_out = out_2.rearrange("z q c -> (z q) c").bitcast(I32)
 
-        def fetch_weighted(t):
-            for d in range(D):
+        def fetch(t):
+            for d in (0, 1):
                 nc.vector.tensor_tensor(terms[t][:, d, :], y[t][:].indirect(pos_sb[d][:]), gate_sb[:, d, :], ALU.mult)
+            for d in (2, 3):
+                nc.scalar.activation(terms[t][:, d, :], y[t][:].indirect(pos_sb[d][:]), ACT.Copy)
 
-        def fetch(t, first, count):
-            cols = slice(first, first + count)
+        def weigh(t):
+            nc.vector.tensor_tensor(terms[t][:, 2:D, :], terms[t][:, 2:D, :], gate_sb[:, 2:D, :], ALU.mult)
+
+        def add_turned(t):
             for d in range(D):
-                nc.scalar.activation(terms[t][:, d, cols], y[t][:].indirect(entries(pos_sb[d], first, count)), ACT.Copy)
+                for b in range(V // P):
+                    cols = slice(b * P, (b + 1) * P)
+                    nc.tensor.matmul(
+                        banks[t][:, cols],
+                        terms[t][:, d, cols],
+                        identity[:],
+                        start=d == 0 and b == 0,
+                        stop=d == D - 1 and b == V // P - 1,
+                        is_transpose=True,
+                    )
 
-        def weigh(t, first, count):
-            cols = slice(first, first + count)
-            nc.vector.tensor_tensor(terms[t][:, :, cols], terms[t][:, :, cols], gate_sb[:, :, cols], ALU.mult)
+        def turn_back(t):
+            nc.scalar.copy(turned[t][:], banks[t][:])
+            for b in range(V // P):
+                cols = slice(b * P, (b + 1) * P)
+                nc.tensor.transpose(banks[4 + t][:, cols], turned[t][:, cols], identity[:])
 
-        def add_up(t, first, count):
-            cols = slice(first, first + count)
-            nc.vector.tensor_tensor(pairs[t % 2][:, :, cols], terms[t][:, 0:2, cols], terms[t][:, 2:D, cols], ALU.add)
-            for half in range(first // HALF, (first + count) // HALF):
-                part = slice(half * HALF, (half + 1) * HALF)
-                nc.vector.tensor_tensor(result[half][:, t, :], pairs[t % 2][:, 0, part], pairs[t % 2][:, 1, part], ALU.add)
-                nc.sync.dma_start(out_rows[:, t, part], result[half][:, t, :])
+        def result_out(t):
+            nc.scalar.copy(result[:, t, :], banks[4 + t][:])
+            nc.sync.dma_start(out_rows[:, t, :], result[:, t, :])
 
-        def hand_on(half):
+        fetch(0)
+        for t in range(1, PACK):
+            nc.scalar.copy(*y_out(t, 1))
+            nc.scalar.copy(*y_out(t, 0))
+            fetch(t)
+            weigh(t - 1)
+            add_turned(t - 1)
+        last = PACK - 1
+        nc.vector.tensor_tensor(pairs[:, 0, :], terms[last][:, 0, :], terms[last][:, 1, :], ALU.add)
+        for t in range(last):
+            turn_back(t)
+        weigh(last)
+        nc.vector.tensor_tensor(pairs[:, 1, :], terms[last][:, 2, :], terms[last][:, 3, :], ALU.add)
+        nc.vector.tensor_tensor(result[:, last, :], pairs[:, 0, :], pairs[:, 1, :], ALU.add)
+        nc.sync.dma_start(out_rows[:, last, :], result[:, last, :])
+        for t in range(last):
+            result_out(t)
+        split = ROUND_VECTOR_COLUMNS
+        nc.vector.tensor_copy(*woven(o_grouped[:, 0 : PACK * split], result[:, :, 0:split]))
+        nc.scalar.copy(*woven(o_grouped[:, PACK * split : PACK * V], result[:, :, split:V]))
+        for half in (0, 1):
             part = slice(half * HALF, (half + 1) * HALF)
-            quantize(o_codes[:, part], o_scales[:, part], o_grouped[half][:])
-            nc.sync.dma_start(words_out[:, part], o_codes[:, part].bitcast(I32))
-
-        nc.vector.tensor_copy(y[0][:, BANK:U], banks[0][:])
-        fetch_weighted(0)
-        add_up(0, 0, V)
-        for t in (1, 2):
-            nc.scalar.copy(y[t][:, BANK:U], banks[t][:])
-            fetch(t, 0, V)
-            weigh(t, 0, V)
-            add_up(t, 0, V)
-        nc.scalar.copy(y[3][:, BANK:U], banks[3][:])
-        fetch(3, 0, HALF)
-        fetch(3, HALF, HALF)
-        weigh(3, 0, HALF)
-        add_up(3, 0, HALF)
-        nc.scalar.copy(*woven(o_grouped[0][:], result[0][:]))
-        weigh(3, HALF, HALF)
-        add_up(3, HALF, HALF)
-        nc.vector.tensor_copy(*woven(o_grouped[1][:], result[1][:]))
-        hand_on(0)
-        hand_on(1)
+            quantize(o_codes[:, part], o_scales[:, part], o_grouped[:, PACK * half * HALF : PACK * (half + 1) * HALF])
+            nc.scalar.dma_start(words_out[:, part], o_codes[:, part].bitcast(I32))
         for q in range(4):
             queue = nc.scalar if q % 2 else nc.sync
             queue.dma_start(scales_out[4 * q : 4 * q + 4, :], o_scales[32 * q : 32 * q + 4, :].bitcast(I32))

@@ -20,7 +20,7 @@ P = 128
 PACK = 4
 HALF = 256
 BANK = 512
-W1_VECTOR_ROWS = 84
+W1_VECTOR_ROWS = 78
 ROUND_VECTOR_COLUMNS = 320
 
 
@@ -103,7 +103,7 @@ def tile_picked_devox_none_lo_kernel(
         x_scales = sb.tile([P, S], U8, name="x_scales", align_bytes=64)
         quantize(x_codes[:], x_scales[:], x_grouped[:].rearrange("p c t -> p (c t)"))
 
-        w1_grouped = sb.tile([P, PACK * H], BF16, name="w1_grouped", align_bytes=64)
+        w1_grouped = sb.tile([P, PACK * H], BF16, name="w1_grouped", tag="w_grouped", align_bytes=64)
         nc.vector.tensor_copy(*dealt(w1_grouped, w1_raw, 0, W1_VECTOR_ROWS))
         nc.scalar.copy(*dealt(w1_grouped, w1_raw, W1_VECTOR_ROWS, P))
         w1_codes = sb.tile([P, H], U32, name="w1_codes", align_bytes=64)
@@ -133,9 +133,9 @@ def tile_picked_devox_none_lo_kernel(
         nc.vector.tensor_copy(up[3][:].indirect(entries(cell_sb, 0, HALF)), h[3][:, 0:HALF])
         scatter_scalar(3, HALF)
 
-        w2_dealt = w2_raw[:].rearrange("p j (m t) -> p m t j", t=PACK)
-        w2_first = sb.tile([P, H], BF16, name="w2_first", tag="h3", align_bytes=64)
-        nc.scalar.copy(w2_first[:].rearrange("p (m j) -> p m j", j=PACK), w2_dealt[:, :, 0, :])
+        w2_grouped = sb.tile([P, PACK * H], BF16, name="w2_grouped", tag="w_grouped", align_bytes=64)
+        w2_out, w2_in = dealt(w2_grouped, w2_raw, 0, P)
+        nc.gpsimd.tensor_scalar(w2_out, w2_in, 1.0, 0.0, ALU.mult, ALU.add)
         w2_codes = sb.tile([P, H], U32, name="w2_codes", align_bytes=64)
         w2_scales = sb.tile([P, H], U8, name="w2_scales", align_bytes=64)
 
@@ -152,13 +152,11 @@ def tile_picked_devox_none_lo_kernel(
         for t in range(PACK):
             add_emb(t, 0)
             add_emb(t, 1)
-        quantize(w2_codes[:, 0:P], w2_scales[:, 0:P], w2_first[:])
+        quantize(w2_codes[:, 0:P], w2_scales[:, 0:P], w2_grouped[:, 0:H])
         quarters = [slice(0, HALF), slice(HALF, BANK)]
         for i in (0, 1):
             nc.scalar.copy(*woven(z_quarter[i][:], z_planes[0][:, :, quarters[i]]))
         nc.vector.tensor_copy(*woven(z_half[:], z_planes[1][:]))
-        w2_rest = sb.tile([P, (PACK - 1) * H], BF16, name="w2_rest", tag="z_planes0", align_bytes=64)
-        nc.scalar.copy(w2_rest[:].rearrange("p (t m j) -> p m t j", t=PACK - 1, j=PACK), w2_dealt[:, :, 1:PACK, :])
         y = tiles([P, U], F32, "y", PACK)
         quantize(z_codes[0][:, quarters[0]], z_scales[0][:, quarters[0]], z_quarter[0][:])
         product(banks[0][:, 0:HALF], w2_codes, w2_scales, 0, z_codes[0][:, quarters[0]], z_scales[0][:, quarters[0]])
@@ -166,10 +164,10 @@ def tile_picked_devox_none_lo_kernel(
         product(banks[4][:], w2_codes, w2_scales, 0, z_codes[1][:], z_scales[1][:])
         quantize(z_codes[0][:, quarters[1]], z_scales[0][:, quarters[1]], z_quarter[1][:])
         product(banks[3][:, 0:HALF], w2_codes, w2_scales, 0, z_codes[0][:, quarters[1]], z_scales[0][:, quarters[1]])
-        nc.vector.tensor_copy(y[0][:, quarters[0]], banks[0][:, 0:HALF])
-        nc.vector.tensor_copy(y[0][:, BANK:U], banks[4][:])
-        nc.scalar.copy(y[0][:, quarters[1]], banks[3][:, 0:HALF])
-        quantize(w2_codes[:, P:H], w2_scales[:, P:H], w2_rest[:])
+        quantize(w2_codes[:, P:H], w2_scales[:, P:H], w2_grouped[:, H : PACK * H])
+        nc.scalar.copy(y[0][:, quarters[0]], banks[0][:, 0:HALF])
+        nc.scalar.copy(y[0][:, BANK:U], banks[4][:])
+        nc.vector.tensor_copy(y[0][:, quarters[1]], banks[3][:, 0:HALF])
         for t in range(1, PACK):
             for half in (1, 0):
                 product(banks[4 * half + t][:], w2_codes, w2_scales, t, z_codes[half][:], z_scales[half][:])

@@ -20,8 +20,9 @@ P = 128
 PACK = 4
 HALF = 256
 BANK = 512
-W1_VECTOR_ROWS = 78
-ROUND_VECTOR_COLUMNS = 320
+W1_VECTOR_ROWS = 84
+SHARE = 384
+ROUND_SCALAR_COLUMNS = 176
 
 
 def tile_picked_devox_none_lo_kernel(
@@ -51,7 +52,7 @@ def tile_picked_devox_none_lo_kernel(
             cols = slice(t * P, (t + 1) * P)
             nc.tensor.matmul_mx(
                 out=bank,
-                lhsT=w_codes[:, cols].bitcast(FP8X4),
+                lhsT=w_codes.bitcast(FP8X4),
                 lhsT_scale=w_scales[:, cols],
                 rhs=codes.bitcast(FP8X4),
                 rhs_scale=scales,
@@ -71,10 +72,11 @@ def tile_picked_devox_none_lo_kernel(
                 planes.rearrange("p t (c i) -> p c t i", i=4),
             )
 
-        offs_sb = load_list(offs, "offs")
         x_rows = xT.rearrange("(p t) c -> t p c", t=PACK)
         x_sb = tiles([P, T], F32, "x", PACK)
-        for t in range(PACK):
+        nc.sync.dma_start(x_sb[0][:], x_rows[0])
+        offs_sb = load_list(offs, "offs")
+        for t in range(1, PACK):
             nc.sync.dma_start(x_sb[t][:], x_rows[t])
         w1_raw = sb.tile([P, PACK, H], F32, name="w1_raw")
         nc.sync.dma_start(w1_raw[:], w1.rearrange("(p j) c -> p j c", j=PACK))
@@ -97,8 +99,12 @@ def tile_picked_devox_none_lo_kernel(
         make_identity(nc, identity[:])
 
         x_grouped = sb.tile([P, S, PACK], BF16, name="x_grouped", align_bytes=64)
+        last = PACK - 1
+        x_picked = tiles([P, HALF], BF16, "x_picked", PACK)
         for t in range(PACK):
-            nc.vector.tensor_copy(x_grouped[:, :, t], x_sb[t][:].indirect(offs_sb[:]))
+            nc.scalar.activation(x_picked[t][:], x_sb[t][:].indirect(entries(offs_sb, 0, HALF)), ACT.Copy)
+            nc.vector.tensor_copy(x_grouped[:, HALF:S, t], x_sb[t][:].indirect(entries(offs_sb, HALF, HALF)))
+            nc.vector.tensor_copy(x_grouped[:, 0:HALF, t], x_picked[t][:])
         x_codes = sb.tile([P, S], U32, name="x_codes", align_bytes=64)
         x_scales = sb.tile([P, S], U8, name="x_scales", align_bytes=64)
         quantize(x_codes[:], x_scales[:], x_grouped[:].rearrange("p c t -> p (c t)"))
@@ -112,31 +118,33 @@ def tile_picked_devox_none_lo_kernel(
         for t in range(PACK):
             cols = slice(t * P, (t + 1) * P)
             quantize(w1_codes[:, cols], w1_scales[:, cols], w1_grouped[:, t * H : (t + 1) * H])
-            product(banks[t][:], w1_codes, w1_scales, t, x_codes[:], x_scales[:])
+            product(banks[t][:], w1_codes[:, cols], w1_scales, t, x_codes[:], x_scales[:])
 
         h = tiles([P, S], F32, "h", PACK)
 
-        def scatter_scalar(t, first):
+        def scatter_scalar(t, first, count=HALF):
             nc.scalar.activation(
-                up[t][:].indirect(entries(cell_sb, first, HALF)), h[t][:, first : first + HALF], ACT.Copy
+                up[t][:].indirect(entries(cell_sb, first, count)), h[t][:, first : first + count], ACT.Copy
             )
 
-        nc.scalar.activation(h[1][:], banks[1][:], ACT.Relu)
-        scatter_scalar(1, 0)
-        scatter_scalar(1, HALF)
         nc.vector.tensor_scalar_max(h[0][:], banks[0][:], 0.0)
         nc.vector.tensor_copy(up[0][:].indirect(cell_sb[:]), h[0][:])
-        nc.vector.tensor_scalar_max(h[3][:], banks[3][:], 0.0)
-        nc.scalar.activation(h[2][:], banks[2][:], ACT.Relu)
-        scatter_scalar(2, 0)
-        scatter_scalar(2, HALF)
-        nc.vector.tensor_copy(up[3][:].indirect(entries(cell_sb, 0, HALF)), h[3][:, 0:HALF])
-        scatter_scalar(3, HALF)
+        nc.vector.tensor_scalar_max(h[3][:, 0:SHARE], banks[3][:, 0:SHARE], 0.0)
+        nc.vector.tensor_copy(up[3][:].indirect(entries(cell_sb, 0, SHARE)), h[3][:, 0:SHARE])
+        for t in (1, 2):
+            nc.scalar.activation(h[t][:], banks[t][:], ACT.Relu)
+        for t in (1, 2):
+            scatter_scalar(t, 0)
+        h_rest = h[2][:, 0 : S - SHARE]
+        nc.scalar.activation(h_rest, banks[3][:, SHARE:S], ACT.Relu)
+        for t in (1, 2):
+            scatter_scalar(t, HALF)
+        nc.scalar.activation(up[3][:].indirect(entries(cell_sb, SHARE, S - SHARE)), h_rest, ACT.Copy)
 
         w2_grouped = sb.tile([P, PACK * H], BF16, name="w2_grouped", tag="w_grouped", align_bytes=64)
         w2_out, w2_in = dealt(w2_grouped, w2_raw, 0, P)
         nc.gpsimd.tensor_scalar(w2_out, w2_in, 1.0, 0.0, ALU.mult, ALU.add)
-        w2_codes = sb.tile([P, H], U32, name="w2_codes", align_bytes=64)
+        w2_codes = sb.tile([P, 2 * P], U32, name="w2_codes", align_bytes=64)
         w2_scales = sb.tile([P, H], U8, name="w2_scales", align_bytes=64)
 
         z_planes = tiles([P, PACK, BANK], BF16, "z_planes", 2)
@@ -147,37 +155,40 @@ def tile_picked_devox_none_lo_kernel(
 
         def add_emb(t, half):
             cols = slice(half * BANK, (half + 1) * BANK)
-            nc.vector.tensor_tensor(z_planes[half][:, t, :], up[t][:, cols], emb_sb[t][:, cols], ALU.add)
+            engine = nc.gpsimd if t == 0 else nc.vector
+            engine.tensor_tensor(z_planes[half][:, t, :], up[t][:, cols], emb_sb[t][:, cols], ALU.add)
 
         for t in range(PACK):
             add_emb(t, 0)
             add_emb(t, 1)
-        quantize(w2_codes[:, 0:P], w2_scales[:, 0:P], w2_grouped[:, 0:H])
+        quantize(w2_codes[:], w2_scales[:, 0 : 2 * P], w2_grouped[:, 0 : 2 * H])
         quarters = [slice(0, HALF), slice(HALF, BANK)]
         for i in (0, 1):
             nc.scalar.copy(*woven(z_quarter[i][:], z_planes[0][:, :, quarters[i]]))
         nc.vector.tensor_copy(*woven(z_half[:], z_planes[1][:]))
         y = tiles([P, U], F32, "y", PACK)
         quantize(z_codes[0][:, quarters[0]], z_scales[0][:, quarters[0]], z_quarter[0][:])
-        product(banks[0][:, 0:HALF], w2_codes, w2_scales, 0, z_codes[0][:, quarters[0]], z_scales[0][:, quarters[0]])
+        product(banks[0][:, 0:HALF], w2_codes[:, 0:P], w2_scales, 0, z_codes[0][:, quarters[0]], z_scales[0][:, quarters[0]])
         quantize(z_codes[1][:], z_scales[1][:], z_half[:])
-        product(banks[4][:], w2_codes, w2_scales, 0, z_codes[1][:], z_scales[1][:])
+        product(banks[4][:], w2_codes[:, 0:P], w2_scales, 0, z_codes[1][:], z_scales[1][:])
         quantize(z_codes[0][:, quarters[1]], z_scales[0][:, quarters[1]], z_quarter[1][:])
-        product(banks[3][:, 0:HALF], w2_codes, w2_scales, 0, z_codes[0][:, quarters[1]], z_scales[0][:, quarters[1]])
-        quantize(w2_codes[:, P:H], w2_scales[:, P:H], w2_grouped[:, H : PACK * H])
+        product(banks[3][:, 0:HALF], w2_codes[:, 0:P], w2_scales, 0, z_codes[0][:, quarters[1]], z_scales[0][:, quarters[1]])
+        w2_late = sb.tile([P, 2 * P], U32, name="w2_late", tag="z_quarter0", align_bytes=64)
+        quantize(w2_late[:], w2_scales[:, 2 * P : H], w2_grouped[:, 2 * H : PACK * H])
+        w2_tile = [(w2_codes, w2_late)[t // 2][:, (t % 2) * P : (t % 2 + 1) * P] for t in range(PACK)]
         nc.scalar.copy(y[0][:, quarters[0]], banks[0][:, 0:HALF])
         nc.scalar.copy(y[0][:, BANK:U], banks[4][:])
         nc.vector.tensor_copy(y[0][:, quarters[1]], banks[3][:, 0:HALF])
         for t in range(1, PACK):
             for half in (1, 0):
-                product(banks[4 * half + t][:], w2_codes, w2_scales, t, z_codes[half][:], z_scales[half][:])
+                product(banks[4 * half + t][:], w2_tile[t], w2_scales, t, z_codes[half][:], z_scales[half][:])
 
         def y_out(t, half):
             return y[t][:, half * BANK : (half + 1) * BANK], banks[4 * half + t][:]
 
         terms = tiles([P, D, V], F32, "terms", PACK)
         pairs = sb.tile([P, 2, V], F32, name="pairs")
-        turned = tiles([P, V], F32, "turned", PACK - 1)
+        turned = [terms[last - 1][:, d, :] for d in (2, 3, 0)]
         result = sb.tile([P, PACK, V], F32, name="result")
         out_rows = out_0.rearrange("(p t) v -> p t v", t=PACK)
         o_grouped = sb.tile([P, PACK * V], BF16, name="o_grouped", align_bytes=64)
@@ -186,10 +197,11 @@ def tile_picked_devox_none_lo_kernel(
         words_out = out_1.rearrange("z p c r -> p (z c r)").bitcast(I32)
         scales_out = out_2.rearrange("z q c -> (z q) c").bitcast(I32)
 
-        def fetch(t):
-            for d in (0, 1):
-                nc.vector.tensor_tensor(terms[t][:, d, :], y[t][:].indirect(pos_sb[d][:]), gate_sb[:, d, :], ALU.mult)
-            for d in (2, 3):
+        def fetch_weighted(t, d):
+            nc.vector.tensor_tensor(terms[t][:, d, :], y[t][:].indirect(pos_sb[d][:]), gate_sb[:, d, :], ALU.mult)
+
+        def fetch(t, which=(2, 3)):
+            for d in which:
                 nc.scalar.activation(terms[t][:, d, :], y[t][:].indirect(pos_sb[d][:]), ACT.Copy)
 
         def weigh(t):
@@ -208,38 +220,57 @@ def tile_picked_devox_none_lo_kernel(
                         is_transpose=True,
                     )
 
+        def back_bank(t, half):
+            return banks[4 + t + half * (t == last - 1)][:, half * HALF : (half + 1) * HALF]
+
         def turn_back(t):
-            nc.scalar.copy(turned[t][:], banks[t][:])
+            nc.scalar.copy(turned[t], banks[t][:])
             for b in range(V // P):
-                cols = slice(b * P, (b + 1) * P)
-                nc.tensor.transpose(banks[4 + t][:, cols], turned[t][:, cols], identity[:])
+                into = back_bank(t, b // 2)[:, (b % 2) * P : (b % 2 + 1) * P]
+                nc.tensor.transpose(into, turned[t][:, b * P : (b + 1) * P], identity[:])
 
-        def result_out(t):
-            nc.scalar.copy(result[:, t, :], banks[4 + t][:])
-            nc.sync.dma_start(out_rows[:, t, :], result[:, t, :])
-
-        fetch(0)
-        for t in range(1, PACK):
+        halves = [slice(0, HALF), slice(HALF, V)]
+        for d in (0, 1):
+            fetch_weighted(0, d)
+        for t in range(1, last):
             nc.scalar.copy(*y_out(t, 1))
             nc.scalar.copy(*y_out(t, 0))
-            fetch(t)
+            fetch(t - 1)
+            for d in (0, 1):
+                fetch_weighted(t, d)
             weigh(t - 1)
             add_turned(t - 1)
-        last = PACK - 1
+        fetch(last - 1)
+        weigh(last - 1)
+        add_turned(last - 1)
+        nc.scalar.copy(*y_out(last, 1))
+        nc.scalar.copy(*y_out(last, 0))
+        fetch(last)
+        for d in (0, 1):
+            fetch_weighted(last, d)
         nc.vector.tensor_tensor(pairs[:, 0, :], terms[last][:, 0, :], terms[last][:, 1, :], ALU.add)
         for t in range(last):
             turn_back(t)
         weigh(last)
-        nc.vector.tensor_tensor(pairs[:, 1, :], terms[last][:, 2, :], terms[last][:, 3, :], ALU.add)
-        nc.vector.tensor_tensor(result[:, last, :], pairs[:, 0, :], pairs[:, 1, :], ALU.add)
+        for half in (1, 0):
+            part = halves[half]
+            nc.vector.tensor_tensor(pairs[:, 1, part], terms[last][:, 2, part], terms[last][:, 3, part], ALU.add)
+        for half in (1, 0):
+            part = halves[half]
+            nc.vector.tensor_tensor(result[:, last, part], pairs[:, 0, part], pairs[:, 1, part], ALU.add)
         nc.sync.dma_start(out_rows[:, last, :], result[:, last, :])
-        for t in range(last):
-            result_out(t)
-        split = ROUND_VECTOR_COLUMNS
-        nc.vector.tensor_copy(*woven(o_grouped[:, 0 : PACK * split], result[:, :, 0:split]))
-        nc.scalar.copy(*woven(o_grouped[:, PACK * split : PACK * V], result[:, :, split:V]))
-        for half in (0, 1):
-            part = slice(half * HALF, (half + 1) * HALF)
+        for t in range(last - 1):
+            nc.scalar.copy(result[:, t, :], banks[4 + t][:])
+            nc.sync.dma_start(out_rows[:, t, :], result[:, t, :])
+        nc.scalar.copy(result[:, last - 1, halves[0]], back_bank(last - 1, 0))
+        nc.vector.tensor_copy(result[:, last - 1, halves[1]], back_bank(last - 1, 1))
+        nc.sync.dma_start(out_rows[:, last - 1, :], result[:, last - 1, :])
+        split = ROUND_SCALAR_COLUMNS
+        nc.scalar.copy(*woven(o_grouped[:, 0 : PACK * split], result[:, :, 0:split]))
+        nc.vector.tensor_copy(*woven(o_grouped[:, PACK * HALF : PACK * V], result[:, :, halves[1]]))
+        nc.vector.tensor_copy(*woven(o_grouped[:, PACK * split : PACK * HALF], result[:, :, split:HALF]))
+        for half in (1, 0):
+            part = halves[half]
             quantize(o_codes[:, part], o_scales[:, part], o_grouped[:, PACK * half * HALF : PACK * (half + 1) * HALF])
             nc.scalar.dma_start(words_out[:, part], o_codes[:, part].bitcast(I32))
         for q in range(4):

@@ -18,10 +18,12 @@ ALU = mybir.AluOpType
 
 P = 128
 PACK = 4
-HALF = 256
+LAST = PACK - 1
 BANK = 512
-W1_VECTOR_ROWS = 84
-SHARE = 384
+HALF = 256
+RUN = 4
+W1_VECTOR_GROUPS = 84
+SCATTER_VECTOR = 384
 ROUND_SCALAR_COLUMNS = 176
 
 
@@ -49,11 +51,10 @@ def tile_picked_devox_none_lo_kernel(
             nc.vector.quantize_mx(out=codes.bitcast(FP8X4), scales=scales, in_=grouped)
 
         def product(bank, w_codes, w_scales, t, codes, scales):
-            cols = slice(t * P, (t + 1) * P)
             nc.tensor.matmul_mx(
                 out=bank,
                 lhsT=w_codes.bitcast(FP8X4),
-                lhsT_scale=w_scales[:, cols],
+                lhsT_scale=w_scales[:, t * P : (t + 1) * P],
                 rhs=codes.bitcast(FP8X4),
                 rhs_scale=scales,
                 start=True,
@@ -66,10 +67,10 @@ def tile_picked_devox_none_lo_kernel(
                 raw[:].rearrange("p j (m t) -> p m t j", t=PACK)[:, m0:m1],
             )
 
-        def woven(grouped, planes):
+        def grouping(grouped, rows):
             return (
-                grouped.rearrange("p (c i t) -> p c t i", i=4, t=PACK),
-                planes.rearrange("p t (c i) -> p c t i", i=4),
+                grouped.rearrange("p (c i t) -> p c t i", i=RUN, t=PACK),
+                rows.rearrange("p t (c i) -> p c t i", i=RUN),
             )
 
         x_rows = xT.rearrange("(p t) c -> t p c", t=PACK)
@@ -91,15 +92,14 @@ def tile_picked_devox_none_lo_kernel(
         gate_sb = sb.tile([P, D, V], F32, name="gate_sb")
         nc.sync.dma_start(gate_sb[:], gate.rearrange("d p v -> p d v"))
 
-        up = tiles([P, U], F32, "up", PACK)
+        cells = tiles([P, U], F32, "cells", PACK)
         for t in range(PACK):
-            nc.gpsimd.memset(up[t][:], 0.0)
+            nc.gpsimd.memset(cells[t][:], 0.0)
 
         identity = sb.tile([P, P], F32, name="identity")
         make_identity(nc, identity[:])
 
         x_grouped = sb.tile([P, S, PACK], BF16, name="x_grouped", align_bytes=64)
-        last = PACK - 1
         x_picked = tiles([P, HALF], BF16, "x_picked", PACK)
         for t in range(PACK):
             nc.scalar.activation(x_picked[t][:], x_sb[t][:].indirect(entries(offs_sb, 0, HALF)), ACT.Copy)
@@ -110,85 +110,86 @@ def tile_picked_devox_none_lo_kernel(
         quantize(x_codes[:], x_scales[:], x_grouped[:].rearrange("p c t -> p (c t)"))
 
         w1_grouped = sb.tile([P, PACK * H], BF16, name="w1_grouped", tag="w_grouped", align_bytes=64)
-        nc.vector.tensor_copy(*dealt(w1_grouped, w1_raw, 0, W1_VECTOR_ROWS))
-        nc.scalar.copy(*dealt(w1_grouped, w1_raw, W1_VECTOR_ROWS, P))
+        nc.vector.tensor_copy(*dealt(w1_grouped, w1_raw, 0, W1_VECTOR_GROUPS))
+        nc.scalar.copy(*dealt(w1_grouped, w1_raw, W1_VECTOR_GROUPS, P))
         w1_codes = sb.tile([P, H], U32, name="w1_codes", align_bytes=64)
         w1_scales = sb.tile([P, H], U8, name="w1_scales", align_bytes=64)
-        banks = [ps.tile([P, BANK], F32, name="bank" + str(b)) for b in range(8)]
+        banks = [ps.tile([P, BANK], F32, name="bank" + str(b)) for b in range(2 * PACK)]
         for t in range(PACK):
             cols = slice(t * P, (t + 1) * P)
             quantize(w1_codes[:, cols], w1_scales[:, cols], w1_grouped[:, t * H : (t + 1) * H])
             product(banks[t][:], w1_codes[:, cols], w1_scales, t, x_codes[:], x_scales[:])
 
         h = tiles([P, S], F32, "h", PACK)
+        nc.vector.tensor_scalar_max(h[0][:], banks[0][:], 0.0)
+        nc.vector.tensor_copy(cells[0][:].indirect(cell_sb[:]), h[0][:])
+        h_most = h[LAST][:, 0:SCATTER_VECTOR]
+        nc.vector.tensor_scalar_max(h_most, banks[LAST][:, 0:SCATTER_VECTOR], 0.0)
+        nc.vector.tensor_copy(cells[LAST][:].indirect(entries(cell_sb, 0, SCATTER_VECTOR)), h_most)
 
-        def scatter_scalar(t, first, count=HALF):
+        def scatter_half(t, first):
             nc.scalar.activation(
-                up[t][:].indirect(entries(cell_sb, first, count)), h[t][:, first : first + count], ACT.Copy
+                cells[t][:].indirect(entries(cell_sb, first, HALF)), h[t][:, first : first + HALF], ACT.Copy
             )
 
-        nc.vector.tensor_scalar_max(h[0][:], banks[0][:], 0.0)
-        nc.vector.tensor_copy(up[0][:].indirect(cell_sb[:]), h[0][:])
-        nc.vector.tensor_scalar_max(h[3][:, 0:SHARE], banks[3][:, 0:SHARE], 0.0)
-        nc.vector.tensor_copy(up[3][:].indirect(entries(cell_sb, 0, SHARE)), h[3][:, 0:SHARE])
-        for t in (1, 2):
+        scalar_tiles = (1, 2)
+        for t in scalar_tiles:
             nc.scalar.activation(h[t][:], banks[t][:], ACT.Relu)
-        for t in (1, 2):
-            scatter_scalar(t, 0)
-        h_rest = h[2][:, 0 : S - SHARE]
-        nc.scalar.activation(h_rest, banks[3][:, SHARE:S], ACT.Relu)
-        for t in (1, 2):
-            scatter_scalar(t, HALF)
-        nc.scalar.activation(up[3][:].indirect(entries(cell_sb, SHARE, S - SHARE)), h_rest, ACT.Copy)
+        for t in scalar_tiles:
+            scatter_half(t, 0)
+        rest = S - SCATTER_VECTOR
+        h_rest = h[2][:, 0:rest]
+        nc.scalar.activation(h_rest, banks[LAST][:, SCATTER_VECTOR:S], ACT.Relu)
+        for t in scalar_tiles:
+            scatter_half(t, HALF)
+        nc.scalar.activation(cells[LAST][:].indirect(entries(cell_sb, SCATTER_VECTOR, rest)), h_rest, ACT.Copy)
 
         w2_grouped = sb.tile([P, PACK * H], BF16, name="w2_grouped", tag="w_grouped", align_bytes=64)
-        w2_out, w2_in = dealt(w2_grouped, w2_raw, 0, P)
-        nc.gpsimd.tensor_scalar(w2_out, w2_in, 1.0, 0.0, ALU.mult, ALU.add)
-        w2_codes = sb.tile([P, 2 * P], U32, name="w2_codes", align_bytes=64)
+        nc.gpsimd.tensor_scalar(*dealt(w2_grouped, w2_raw, 0, P), 1.0, 0.0, ALU.mult, ALU.add)
+        w2_early = sb.tile([P, 2 * P], U32, name="w2_early", align_bytes=64)
         w2_scales = sb.tile([P, H], U8, name="w2_scales", align_bytes=64)
 
-        z_planes = tiles([P, PACK, BANK], BF16, "z_planes", 2)
+        z_rows = tiles([P, PACK, BANK], BF16, "z_rows", 2)
         z_quarter = tiles([P, PACK * HALF], BF16, "z_quarter", 2)
-        z_half = sb.tile([P, PACK * BANK], BF16, name="z_half", align_bytes=64)
+        z_upper = sb.tile([P, PACK * BANK], BF16, name="z_upper", align_bytes=64)
         z_codes = tiles([P, BANK], U32, "z_codes", 2)
         z_scales = tiles([P, BANK], U8, "z_scales", 2)
-
-        def add_emb(t, half):
-            cols = slice(half * BANK, (half + 1) * BANK)
-            engine = nc.gpsimd if t == 0 else nc.vector
-            engine.tensor_tensor(z_planes[half][:, t, :], up[t][:, cols], emb_sb[t][:, cols], ALU.add)
-
         for t in range(PACK):
-            add_emb(t, 0)
-            add_emb(t, 1)
-        quantize(w2_codes[:], w2_scales[:, 0 : 2 * P], w2_grouped[:, 0 : 2 * H])
-        quarters = [slice(0, HALF), slice(HALF, BANK)]
+            adder = nc.gpsimd if t == 0 else nc.vector
+            for half in (0, 1):
+                cols = slice(half * BANK, (half + 1) * BANK)
+                adder.tensor_tensor(z_rows[half][:, t, :], cells[t][:, cols], emb_sb[t][:, cols], ALU.add)
+        quantize(w2_early[:], w2_scales[:, 0 : 2 * P], w2_grouped[:, 0 : 2 * H])
+        halves = [slice(0, HALF), slice(HALF, 2 * HALF)]
         for i in (0, 1):
-            nc.scalar.copy(*woven(z_quarter[i][:], z_planes[0][:, :, quarters[i]]))
-        nc.vector.tensor_copy(*woven(z_half[:], z_planes[1][:]))
+            nc.scalar.copy(*grouping(z_quarter[i][:], z_rows[0][:, :, halves[i]]))
+        nc.vector.tensor_copy(*grouping(z_upper[:], z_rows[1][:]))
+
         y = tiles([P, U], F32, "y", PACK)
-        quantize(z_codes[0][:, quarters[0]], z_scales[0][:, quarters[0]], z_quarter[0][:])
-        product(banks[0][:, 0:HALF], w2_codes[:, 0:P], w2_scales, 0, z_codes[0][:, quarters[0]], z_scales[0][:, quarters[0]])
-        quantize(z_codes[1][:], z_scales[1][:], z_half[:])
-        product(banks[4][:], w2_codes[:, 0:P], w2_scales, 0, z_codes[1][:], z_scales[1][:])
-        quantize(z_codes[0][:, quarters[1]], z_scales[0][:, quarters[1]], z_quarter[1][:])
-        product(banks[3][:, 0:HALF], w2_codes[:, 0:P], w2_scales, 0, z_codes[0][:, quarters[1]], z_scales[0][:, quarters[1]])
+        z_parts = (
+            (z_quarter[0][:], z_codes[0][:, halves[0]], z_scales[0][:, halves[0]], banks[0][:, 0:HALF]),
+            (z_upper[:], z_codes[1][:], z_scales[1][:], banks[PACK][:]),
+            (z_quarter[1][:], z_codes[0][:, halves[1]], z_scales[0][:, halves[1]], banks[LAST][:, 0:HALF]),
+        )
+        for grouped, codes, scales, bank in z_parts:
+            quantize(codes, scales, grouped)
+            product(bank, w2_early[:, 0:P], w2_scales, 0, codes, scales)
         w2_late = sb.tile([P, 2 * P], U32, name="w2_late", tag="z_quarter0", align_bytes=64)
         quantize(w2_late[:], w2_scales[:, 2 * P : H], w2_grouped[:, 2 * H : PACK * H])
-        w2_tile = [(w2_codes, w2_late)[t // 2][:, (t % 2) * P : (t % 2 + 1) * P] for t in range(PACK)]
-        nc.scalar.copy(y[0][:, quarters[0]], banks[0][:, 0:HALF])
-        nc.scalar.copy(y[0][:, BANK:U], banks[4][:])
-        nc.vector.tensor_copy(y[0][:, quarters[1]], banks[3][:, 0:HALF])
+        nc.scalar.copy(y[0][:, halves[0]], banks[0][:, 0:HALF])
+        nc.scalar.copy(y[0][:, BANK:U], banks[PACK][:])
+        nc.vector.tensor_copy(y[0][:, halves[1]], banks[LAST][:, 0:HALF])
         for t in range(1, PACK):
+            w2_codes = (w2_early, w2_late)[t // 2][:, (t % 2) * P : (t % 2 + 1) * P]
             for half in (1, 0):
-                product(banks[4 * half + t][:], w2_tile[t], w2_scales, t, z_codes[half][:], z_scales[half][:])
+                product(banks[PACK * half + t][:], w2_codes, w2_scales, t, z_codes[half][:], z_scales[half][:])
 
-        def y_out(t, half):
-            return y[t][:, half * BANK : (half + 1) * BANK], banks[4 * half + t][:]
+        def y_out(t):
+            for half in (1, 0):
+                nc.scalar.copy(y[t][:, half * BANK : (half + 1) * BANK], banks[PACK * half + t][:])
 
         terms = tiles([P, D, V], F32, "terms", PACK)
         pairs = sb.tile([P, 2, V], F32, name="pairs")
-        turned = [terms[last - 1][:, d, :] for d in (2, 3, 0)]
         result = sb.tile([P, PACK, V], F32, name="result")
         out_rows = out_0.rearrange("(p t) v -> p t v", t=PACK)
         o_grouped = sb.tile([P, PACK * V], BF16, name="o_grouped", align_bytes=64)
@@ -197,17 +198,18 @@ def tile_picked_devox_none_lo_kernel(
         words_out = out_1.rearrange("z p c r -> p (z c r)").bitcast(I32)
         scales_out = out_2.rearrange("z q c -> (z q) c").bitcast(I32)
 
-        def fetch_weighted(t, d):
-            nc.vector.tensor_tensor(terms[t][:, d, :], y[t][:].indirect(pos_sb[d][:]), gate_sb[:, d, :], ALU.mult)
+        def fetch_weighted(t):
+            for d in (0, 1):
+                nc.vector.tensor_tensor(terms[t][:, d, :], y[t][:].indirect(pos_sb[d][:]), gate_sb[:, d, :], ALU.mult)
 
-        def fetch(t, which=(2, 3)):
-            for d in which:
+        def fetch_plain(t):
+            for d in (2, 3):
                 nc.scalar.activation(terms[t][:, d, :], y[t][:].indirect(pos_sb[d][:]), ACT.Copy)
 
         def weigh(t):
             nc.vector.tensor_tensor(terms[t][:, 2:D, :], terms[t][:, 2:D, :], gate_sb[:, 2:D, :], ALU.mult)
 
-        def add_turned(t):
+        def add_transposed(t):
             for d in range(D):
                 for b in range(V // P):
                     cols = slice(b * P, (b + 1) * P)
@@ -220,59 +222,54 @@ def tile_picked_devox_none_lo_kernel(
                         is_transpose=True,
                     )
 
-        def back_bank(t, half):
-            return banks[4 + t + half * (t == last - 1)][:, half * HALF : (half + 1) * HALF]
+        summed = [terms[LAST - 1][:, d, :] for d in (2, 3, 0)]
 
-        def turn_back(t):
-            nc.scalar.copy(turned[t], banks[t][:])
+        def back_bank(t, half):
+            return banks[PACK + t + half * (t == LAST - 1)][:, halves[half]]
+
+        def transpose_back(t):
+            nc.scalar.copy(summed[t], banks[t][:])
             for b in range(V // P):
                 into = back_bank(t, b // 2)[:, (b % 2) * P : (b % 2 + 1) * P]
-                nc.tensor.transpose(into, turned[t][:, b * P : (b + 1) * P], identity[:])
+                nc.tensor.transpose(into, summed[t][:, b * P : (b + 1) * P], identity[:])
 
-        halves = [slice(0, HALF), slice(HALF, V)]
-        for d in (0, 1):
-            fetch_weighted(0, d)
-        for t in range(1, last):
-            nc.scalar.copy(*y_out(t, 1))
-            nc.scalar.copy(*y_out(t, 0))
-            fetch(t - 1)
-            for d in (0, 1):
-                fetch_weighted(t, d)
+        fetch_weighted(0)
+        for t in range(1, LAST):
+            y_out(t)
+            fetch_plain(t - 1)
+            fetch_weighted(t)
             weigh(t - 1)
-            add_turned(t - 1)
-        fetch(last - 1)
-        weigh(last - 1)
-        add_turned(last - 1)
-        nc.scalar.copy(*y_out(last, 1))
-        nc.scalar.copy(*y_out(last, 0))
-        fetch(last)
-        for d in (0, 1):
-            fetch_weighted(last, d)
-        nc.vector.tensor_tensor(pairs[:, 0, :], terms[last][:, 0, :], terms[last][:, 1, :], ALU.add)
-        for t in range(last):
-            turn_back(t)
-        weigh(last)
-        for half in (1, 0):
-            part = halves[half]
-            nc.vector.tensor_tensor(pairs[:, 1, part], terms[last][:, 2, part], terms[last][:, 3, part], ALU.add)
-        for half in (1, 0):
-            part = halves[half]
-            nc.vector.tensor_tensor(result[:, last, part], pairs[:, 0, part], pairs[:, 1, part], ALU.add)
-        nc.sync.dma_start(out_rows[:, last, :], result[:, last, :])
-        for t in range(last - 1):
-            nc.scalar.copy(result[:, t, :], banks[4 + t][:])
+            add_transposed(t - 1)
+        fetch_plain(LAST - 1)
+        weigh(LAST - 1)
+        add_transposed(LAST - 1)
+
+        y_out(LAST)
+        fetch_plain(LAST)
+        fetch_weighted(LAST)
+        weigh(LAST)
+        nc.vector.tensor_tensor(pairs[:, 0, :], terms[LAST][:, 0, :], terms[LAST][:, 1, :], ALU.add)
+        for t in range(LAST):
+            transpose_back(t)
+        for part in reversed(halves):
+            nc.vector.tensor_tensor(pairs[:, 1, part], terms[LAST][:, 2, part], terms[LAST][:, 3, part], ALU.add)
+        for part in reversed(halves):
+            nc.vector.tensor_tensor(result[:, LAST, part], pairs[:, 0, part], pairs[:, 1, part], ALU.add)
+        for t in range(LAST - 1):
+            nc.scalar.copy(result[:, t, :], banks[PACK + t][:])
             nc.sync.dma_start(out_rows[:, t, :], result[:, t, :])
-        nc.scalar.copy(result[:, last - 1, halves[0]], back_bank(last - 1, 0))
-        nc.vector.tensor_copy(result[:, last - 1, halves[1]], back_bank(last - 1, 1))
-        nc.sync.dma_start(out_rows[:, last - 1, :], result[:, last - 1, :])
+        nc.scalar.copy(result[:, LAST - 1, halves[0]], back_bank(LAST - 1, 0))
+        nc.vector.tensor_copy(result[:, LAST - 1, halves[1]], back_bank(LAST - 1, 1))
+        nc.sync.dma_start(out_rows[:, LAST - 1 : PACK, :], result[:, LAST - 1 : PACK, :])
+
         split = ROUND_SCALAR_COLUMNS
-        nc.scalar.copy(*woven(o_grouped[:, 0 : PACK * split], result[:, :, 0:split]))
-        nc.vector.tensor_copy(*woven(o_grouped[:, PACK * HALF : PACK * V], result[:, :, halves[1]]))
-        nc.vector.tensor_copy(*woven(o_grouped[:, PACK * split : PACK * HALF], result[:, :, split:HALF]))
+        nc.scalar.copy(*grouping(o_grouped[:, 0 : PACK * split], result[:, :, 0:split]))
+        nc.vector.tensor_copy(*grouping(o_grouped[:, PACK * HALF : PACK * V], result[:, :, halves[1]]))
+        nc.vector.tensor_copy(*grouping(o_grouped[:, PACK * split : PACK * HALF], result[:, :, split:HALF]))
         for half in (1, 0):
             part = halves[half]
             quantize(o_codes[:, part], o_scales[:, part], o_grouped[:, PACK * half * HALF : PACK * (half + 1) * HALF])
             nc.scalar.dma_start(words_out[:, part], o_codes[:, part].bitcast(I32))
-        for q in range(4):
+        for q in range(P // 32):
             queue = nc.scalar if q % 2 else nc.sync
             queue.dma_start(scales_out[4 * q : 4 * q + 4, :], o_scales[32 * q : 32 * q + 4, :].bitcast(I32))

from contextlib import ExitStack

import concourse.mybir as mybir
from concourse.masks import make_identity

K, T, S, D, V, H, U = 512, 2048, 512, 4, 512, 512, 1024
FLOPS = 2 * K * H * S + 2 * H * H * U

F32 = mybir.dt.float32
BF16 = mybir.dt.bfloat16
I32 = mybir.dt.int32
U32 = mybir.dt.uint32
U16 = mybir.dt.uint16
U8 = mybir.dt.uint8
FP8X4 = mybir.dt.float8_e4m3fn_x4
ACT = mybir.ActivationFunctionType
ALU = mybir.AluOpType

P = 128
PACK = 4
LAST = PACK - 1
BANK = 512
HALF = 256
RUN = 4
W1_VECTOR_GROUPS = 84
SCATTER_VECTOR = 384
ROUND_SCALAR_COLUMNS = 176


def tile_picked_devox_none_lo_kernel(
    tc, xT, w1, w2, gate, emb, offs, cell, pos1, pos2, pos3, pos4, out_0, out_1, out_2
):
    nc = tc.nc
    with ExitStack() as ctx:
        lists = ctx.enter_context(tc.tile_pool(name="lists", bufs=1))
        sb = ctx.enter_context(tc.tile_pool(name="sb", bufs=1))
        ps = ctx.enter_context(tc.psum_pool(name="ps", bufs=1))

        def load_list(src, name):
            held = lists.tile([P, S // 16], U16, name=name)
            nc.sync.dma_start(held[:], src)
            return held

        def tiles(shape, dtype, name, count):
            return [sb.tile(shape, dtype, name=name + str(i), tag=name + str(i), align_bytes=64) for i in range(count)]

        def entries(held, first, count):
            return held[:, first // 16 : (first + count) // 16]

        def quantize(codes, scales, grouped):
            nc.vector.quantize_mx(out=codes.bitcast(FP8X4), scales=scales, in_=grouped)

        def product(bank, w_codes, w_scales, t, codes, scales):
            nc.tensor.matmul_mx(
                out=bank,
                lhsT=w_codes.bitcast(FP8X4),
                lhsT_scale=w_scales[:, t * P : (t + 1) * P],
                rhs=codes.bitcast(FP8X4),
                rhs_scale=scales,
                start=True,
                stop=True,
            )

        def dealt(grouped, raw, m0, m1):
            return (
                grouped[:].rearrange("p (t m j) -> p m t j", t=PACK, j=PACK)[:, m0:m1],
                raw[:].rearrange("p j (m t) -> p m t j", t=PACK)[:, m0:m1],
            )

        def grouping(grouped, rows):
            return (
                grouped.rearrange("p (c i t) -> p c t i", i=RUN, t=PACK),
                rows.rearrange("p t (c i) -> p c t i", i=RUN),
            )

        x_rows = xT.rearrange("(p t) c -> t p c", t=PACK)
        x_sb = tiles([P, T], F32, "x", PACK)
        nc.sync.dma_start(x_sb[0][:], x_rows[0])
        offs_sb = load_list(offs, "offs")
        for t in range(1, PACK):
            nc.sync.dma_start(x_sb[t][:], x_rows[t])
        w1_raw = sb.tile([P, PACK, H], F32, name="w1_raw")
        nc.sync.dma_start(w1_raw[:], w1.rearrange("(p j) c -> p j c", j=PACK))
        cell_sb = load_list(cell, "cell")
        w2_raw = sb.tile([P, PACK, H], F32, name="w2_raw")
        nc.sync.dma_start(w2_raw[:], w2.rearrange("(p j) c -> p j c", j=PACK))
        emb_rows = emb.rearrange("(p t) c -> t p c", t=PACK)
        emb_sb = tiles([P, U], F32, "emb", PACK)
        for t in range(PACK):
            nc.sync.dma_start(emb_sb[t][:], emb_rows[t])
        pos_sb = [load_list(src, "pos" + str(d)) for d, src in enumerate((pos1, pos2, pos3, pos4))]
        gate_sb = sb.tile([P, D, V], F32, name="gate_sb")
        nc.sync.dma_start(gate_sb[:], gate.rearrange("d p v -> p d v"))

        cells = tiles([P, U], F32, "cells", PACK)
        for t in range(PACK):
            nc.gpsimd.memset(cells[t][:], 0.0)

        identity = sb.tile([P, P], F32, name="identity")
        make_identity(nc, identity[:])

        x_grouped = sb.tile([P, S, PACK], BF16, name="x_grouped", align_bytes=64)
        x_picked = tiles([P, HALF], BF16, "x_picked", PACK)
        for t in range(PACK):
            nc.scalar.activation(x_picked[t][:], x_sb[t][:].indirect(entries(offs_sb, 0, HALF)), ACT.Copy)
            nc.vector.tensor_copy(x_grouped[:, HALF:S, t], x_sb[t][:].indirect(entries(offs_sb, HALF, HALF)))
            nc.vector.tensor_copy(x_grouped[:, 0:HALF, t], x_picked[t][:])
        x_codes = sb.tile([P, S], U32, name="x_codes", align_bytes=64)
        x_scales = sb.tile([P, S], U8, name="x_scales", align_bytes=64)
        quantize(x_codes[:], x_scales[:], x_grouped[:].rearrange("p c t -> p (c t)"))

        w1_grouped = sb.tile([P, PACK * H], BF16, name="w1_grouped", tag="w_grouped", align_bytes=64)
        nc.vector.tensor_copy(*dealt(w1_grouped, w1_raw, 0, W1_VECTOR_GROUPS))
        nc.scalar.copy(*dealt(w1_grouped, w1_raw, W1_VECTOR_GROUPS, P))
        w1_codes = sb.tile([P, H], U32, name="w1_codes", align_bytes=64)
        w1_scales = sb.tile([P, H], U8, name="w1_scales", align_bytes=64)
        banks = [ps.tile([P, BANK], F32, name="bank" + str(b)) for b in range(2 * PACK)]
        for t in range(PACK):
            cols = slice(t * P, (t + 1) * P)
            quantize(w1_codes[:, cols], w1_scales[:, cols], w1_grouped[:, t * H : (t + 1) * H])
            product(banks[t][:], w1_codes[:, cols], w1_scales, t, x_codes[:], x_scales[:])

        h = tiles([P, S], F32, "h", PACK)
        nc.vector.tensor_scalar_max(h[0][:], banks[0][:], 0.0)
        nc.vector.tensor_copy(cells[0][:].indirect(cell_sb[:]), h[0][:])
        h_most = h[LAST][:, 0:SCATTER_VECTOR]
        nc.vector.tensor_scalar_max(h_most, banks[LAST][:, 0:SCATTER_VECTOR], 0.0)
        nc.vector.tensor_copy(cells[LAST][:].indirect(entries(cell_sb, 0, SCATTER_VECTOR)), h_most)

        def scatter_half(t, first):
            nc.scalar.activation(
                cells[t][:].indirect(entries(cell_sb, first, HALF)), h[t][:, first : first + HALF], ACT.Copy
            )

        scalar_tiles = (1, 2)
        for t in scalar_tiles:
            nc.scalar.activation(h[t][:], banks[t][:], ACT.Relu)
        for t in scalar_tiles:
            scatter_half(t, 0)
        rest = S - SCATTER_VECTOR
        h_rest = h[2][:, 0:rest]
        nc.scalar.activation(h_rest, banks[LAST][:, SCATTER_VECTOR:S], ACT.Relu)
        for t in scalar_tiles:
            scatter_half(t, HALF)
        nc.scalar.activation(cells[LAST][:].indirect(entries(cell_sb, SCATTER_VECTOR, rest)), h_rest, ACT.Copy)

        w2_grouped = sb.tile([P, PACK * H], BF16, name="w2_grouped", tag="w_grouped", align_bytes=64)
        nc.gpsimd.tensor_scalar(*dealt(w2_grouped, w2_raw, 0, P), 1.0, 0.0, ALU.mult, ALU.add)
        w2_early = sb.tile([P, 2 * P], U32, name="w2_early", align_bytes=64)
        w2_scales = sb.tile([P, H], U8, name="w2_scales", align_bytes=64)

        z_rows = tiles([P, PACK, BANK], BF16, "z_rows", 2)
        z_quarter = tiles([P, PACK * HALF], BF16, "z_quarter", 2)
        z_upper = sb.tile([P, PACK * BANK], BF16, name="z_upper", align_bytes=64)
        z_codes = tiles([P, BANK], U32, "z_codes", 2)
        z_scales = tiles([P, BANK], U8, "z_scales", 2)
        for t in range(PACK):
            adder = nc.gpsimd if t == 0 else nc.vector
            for half in (0, 1):
                cols = slice(half * BANK, (half + 1) * BANK)
                adder.tensor_tensor(z_rows[half][:, t, :], cells[t][:, cols], emb_sb[t][:, cols], ALU.add)
        quantize(w2_early[:], w2_scales[:, 0 : 2 * P], w2_grouped[:, 0 : 2 * H])
        halves = [slice(0, HALF), slice(HALF, 2 * HALF)]
        for i in (0, 1):
            nc.scalar.copy(*grouping(z_quarter[i][:], z_rows[0][:, :, halves[i]]))
        nc.vector.tensor_copy(*grouping(z_upper[:], z_rows[1][:]))

        y = tiles([P, U], F32, "y", PACK)
        z_parts = (
            (z_quarter[0][:], z_codes[0][:, halves[0]], z_scales[0][:, halves[0]], banks[0][:, 0:HALF]),
            (z_upper[:], z_codes[1][:], z_scales[1][:], banks[PACK][:]),
            (z_quarter[1][:], z_codes[0][:, halves[1]], z_scales[0][:, halves[1]], banks[LAST][:, 0:HALF]),
        )
        for grouped, codes, scales, bank in z_parts:
            quantize(codes, scales, grouped)
            product(bank, w2_early[:, 0:P], w2_scales, 0, codes, scales)
        w2_late = sb.tile([P, 2 * P], U32, name="w2_late", tag="z_quarter0", align_bytes=64)
        quantize(w2_late[:], w2_scales[:, 2 * P : H], w2_grouped[:, 2 * H : PACK * H])
        nc.scalar.copy(y[0][:, halves[0]], banks[0][:, 0:HALF])
        nc.scalar.copy(y[0][:, BANK:U], banks[PACK][:])
        nc.vector.tensor_copy(y[0][:, halves[1]], banks[LAST][:, 0:HALF])
        for t in range(1, PACK):
            w2_codes = (w2_early, w2_late)[t // 2][:, (t % 2) * P : (t % 2 + 1) * P]
            for half in (1, 0):
                product(banks[PACK * half + t][:], w2_codes, w2_scales, t, z_codes[half][:], z_scales[half][:])

        def y_out(t):
            for half in (1, 0):
                nc.scalar.copy(y[t][:, half * BANK : (half + 1) * BANK], banks[PACK * half + t][:])

        terms = tiles([P, D, V], F32, "terms", PACK)
        pairs = sb.tile([P, 2, V], F32, name="pairs")
        result = sb.tile([P, PACK, V], F32, name="result")
        out_rows = out_0.rearrange("(p t) v -> p t v", t=PACK)
        o_grouped = sb.tile([P, PACK * V], BF16, name="o_grouped", align_bytes=64)
        o_codes = sb.tile([P, V], U32, name="o_codes", align_bytes=64)
        o_scales = sb.tile([P, V], U8, name="o_scales", align_bytes=64)
        words_out = out_1.rearrange("z p c r -> p (z c r)").bitcast(I32)
        scales_out = out_2.rearrange("z q c -> (z q) c").bitcast(I32)

        def fetch_weighted(t):
            for d in (0, 1):
                nc.vector.tensor_tensor(terms[t][:, d, :], y[t][:].indirect(pos_sb[d][:]), gate_sb[:, d, :], ALU.mult)

        def fetch_plain(t):
            for d in (2, 3):
                nc.scalar.activation(terms[t][:, d, :], y[t][:].indirect(pos_sb[d][:]), ACT.Copy)

        def weigh(t):
            nc.vector.tensor_tensor(terms[t][:, 2:D, :], terms[t][:, 2:D, :], gate_sb[:, 2:D, :], ALU.mult)

        def add_transposed(t):
            for d in range(D):
                for b in range(V // P):
                    cols = slice(b * P, (b + 1) * P)
                    nc.tensor.matmul(
                        banks[t][:, cols],
                        terms[t][:, d, cols],
                        identity[:],
                        start=d == 0 and b == 0,
                        stop=d == D - 1 and b == V // P - 1,
                        is_transpose=True,
                    )

        summed = [terms[LAST - 1][:, d, :] for d in (2, 3, 0)]

        def back_bank(t, half):
            return banks[PACK + t + half * (t == LAST - 1)][:, halves[half]]

        def transpose_back(t):
            nc.scalar.copy(summed[t], banks[t][:])
            for b in range(V // P):
                into = back_bank(t, b // 2)[:, (b % 2) * P : (b % 2 + 1) * P]
                nc.tensor.transpose(into, summed[t][:, b * P : (b + 1) * P], identity[:])

        fetch_weighted(0)
        for t in range(1, LAST):
            y_out(t)
            fetch_plain(t - 1)
            fetch_weighted(t)
            weigh(t - 1)
            add_transposed(t - 1)
        fetch_plain(LAST - 1)
        weigh(LAST - 1)
        add_transposed(LAST - 1)

        y_out(LAST)
        fetch_plain(LAST)
        fetch_weighted(LAST)
        weigh(LAST)
        nc.vector.tensor_tensor(pairs[:, 0, :], terms[LAST][:, 0, :], terms[LAST][:, 1, :], ALU.add)
        for t in range(LAST):
            transpose_back(t)
        for part in reversed(halves):
            nc.vector.tensor_tensor(pairs[:, 1, part], terms[LAST][:, 2, part], terms[LAST][:, 3, part], ALU.add)
        for part in reversed(halves):
            nc.vector.tensor_tensor(result[:, LAST, part], pairs[:, 0, part], pairs[:, 1, part], ALU.add)
        for t in range(LAST - 1):
            nc.scalar.copy(result[:, t, :], banks[PACK + t][:])
            nc.sync.dma_start(out_rows[:, t, :], result[:, t, :])
        nc.scalar.copy(result[:, LAST - 1, halves[0]], back_bank(LAST - 1, 0))
        nc.vector.tensor_copy(result[:, LAST - 1, halves[1]], back_bank(LAST - 1, 1))
        nc.sync.dma_start(out_rows[:, LAST - 1 : PACK, :], result[:, LAST - 1 : PACK, :])

        split = ROUND_SCALAR_COLUMNS
        nc.scalar.copy(*grouping(o_grouped[:, 0 : PACK * split], result[:, :, 0:split]))
        nc.vector.tensor_copy(*grouping(o_grouped[:, PACK * HALF : PACK * V], result[:, :, halves[1]]))
        nc.vector.tensor_copy(*grouping(o_grouped[:, PACK * split : PACK * HALF], result[:, :, split:HALF]))
        for half in (1, 0):
            part = halves[half]
            quantize(o_codes[:, part], o_scales[:, part], o_grouped[:, PACK * half * HALF : PACK * (half + 1) * HALF])
            nc.scalar.dma_start(words_out[:, part], o_codes[:, part].bitcast(I32))
        for q in range(P // 32):
            queue = nc.scalar if q % 2 else nc.sync
            queue.dma_start(scales_out[4 * q : 4 * q + 4, :], o_scales[32 * q : 32 * q + 4, :].bitcast(I32))
